import numpy as np
import ml_dtypes


def mxq(x, axis, fmt="e4m3"):
    dtype, down = {"e4m3": (ml_dtypes.float8_e4m3fn, 7), "e5m2": (ml_dtypes.float8_e5m2, 14)}[fmt]
    v = np.moveaxis(np.asarray(x, np.float32).astype(ml_dtypes.bfloat16).astype(np.float64), axis, -1)
    blocks = v.reshape(v.shape[:-1] + (-1, 32))
    amax = np.abs(blocks).max(-1, keepdims=True)
    byte = np.maximum(np.where(amax > 0, np.frexp(amax)[1] - 1 + 127, 0) - down, 1)
    scale = np.exp2(byte - 127.0)
    codes = (blocks / scale).astype(np.float32).astype(dtype).astype(np.float64)
    return np.moveaxis((codes * scale).reshape(v.shape), -1, axis)


WIDE = False


def mx_kscale(k):
    if not WIDE:
        return np.ones(k)
    levels = np.array([10, -10, 5, -5, 0])
    if k % 512:
        return np.exp2(np.random.permutation(np.resize(levels, k // 32))).repeat(32)
    a = np.empty((k // 512, 16))
    for p in range(k // 512):
        a[p, :8] = np.random.permutation(np.resize(levels, 8))
        for g in range(8):
            far = levels[np.abs(levels - a[p, g]) >= 10]
            a[p, g + 8] = far[np.random.randint(len(far))]
    return np.exp2(a.ravel()).repeat(32)


def f64(x):
    return np.asarray(x).astype(np.float64)


def striped(idx):
    return np.tile(idx.reshape(-1, 16).T, (8, 1)).astype(np.uint16)


def unstriped(offs):
    return offs[:16].T.reshape(-1).astype(np.int64)


def striped8(idx):
    return np.concatenate([x.reshape(-1, 16).T for x in idx]).astype(np.uint16)


def runs(offs, k):
    lists = np.stack([offs[16 * r : 16 * r + 16].T.reshape(-1) for r in range(8)]).astype(np.int64)
    return lists[np.arange(k) % 512 // 64]


def pack_weight(w):
    k, n = w.shape
    w = f64(np.asarray(w, np.float32).astype(ml_dtypes.bfloat16)).reshape(k // 32, 32, n)
    amax = np.abs(w).max(1)
    byte = np.clip(np.where(amax > 0, np.frexp(amax)[1] - 1 + 127 - 7, 1), 1, 254)
    scaled = (w * np.exp2(127.0 - byte)[:, None, :]).reshape(k, n).astype(np.float32)
    words = np.ascontiguousarray(scaled.reshape(k // 512, 128, 4, n).transpose(0, 1, 3, 2)).astype(ml_dtypes.float8_e4m3fn).view(np.uint8)
    return words, np.ascontiguousarray(byte.astype(np.uint8).reshape(k // 512, 16, n))


def unpack_weight(words, scales):
    g, p, n, _ = words.shape
    vals = np.ascontiguousarray(words).view(ml_dtypes.float8_e4m3fn).astype(np.float64) * np.repeat(np.exp2(scales.astype(np.float64) - 127.0), 8, axis=1)[..., None]
    return vals.transpose(0, 1, 3, 2).reshape(g * 512, n)


K, T, S, G, H, U = 512, 1024, 512, 2048, 512, 1024


def setup_inputs():
    n = np.random.standard_normal
    s = mx_kscale(K)[:, None]
    packed_xT = pack_weight(n((K, T)) * s)
    packed_dT = pack_weight(n((K, G)) / s)
    return {
        "x_words": packed_xT[0],
        "x_scales": packed_xT[1],
        "d_words": packed_dT[0],
        "d_scales": packed_dT[1],
        "mem": n((H, U)).astype(np.float32),
        "gs": (np.random.uniform(0.5, 1.5, (K, 1)) * s).astype(np.float32),
        "offs": striped(np.random.permutation(T)[:S]),
        "k1": striped8(np.random.randint(0, G, (8, H))),
        "n1": striped8(np.stack([np.random.permutation(U)[:S] for _ in range(8)])),
        "n2": striped8(np.stack([np.random.permutation(U) for _ in range(8)])),
        "k2": striped8(np.random.randint(0, G, (8, H))),
        "n3": striped8(np.stack([np.random.permutation(U) for _ in range(8)])),
        "n4": striped8(np.stack([np.random.permutation(U) for _ in range(8)])),
    }


def reference(x_words, x_scales, d_words, d_scales, mem, gs, offs, k1, n1, n2, k2, n3, n4):
    d_k2 = unpack_weight(d_words, d_scales)[np.arange(K)[:, None], runs(k2, K)]
    d_k1 = unpack_weight(d_words, d_scales)[np.arange(K)[:, None], runs(k1, K)]
    xq = unpack_weight(x_words, x_scales)[:, unstriped(offs)]
    h = 0.0625 * (d_k1.T @ xq)
    pg = f64(mem).copy()
    pg[np.arange(H)[:, None], runs(n1, H)] = h
    z = f64(gs) * (pg - (0.5 * (pg[np.arange(H)[:, None], runs(n2, H)])))
    h2 = 0.0625 * ((d_k2.T @ mxq(z, 0, "e4m3")))
    return h2[np.arange(H)[:, None], runs(n3, H)] - (h2[np.arange(H)[:, None], runs(n4, H)])

@@ -1,0 +1,168 @@
+from contextlib import ExitStack
+
+import concourse.mybir as mybir
+
+K, T, S, G, H, U = 512, 1024, 512, 2048, 512, 1024
+P = 128
+PACK = 4
+FLOPS = 2 * K * H * S + 2 * K * H * U
+
+F32 = mybir.dt.float32
+BF16 = mybir.dt.bfloat16
+I32 = mybir.dt.int32
+U32 = mybir.dt.uint32
+U16 = mybir.dt.uint16
+U8 = mybir.dt.uint8
+FP8X4 = mybir.dt.float8_e4m3fn_x4
+COPY = mybir.ActivationFunctionType.Copy
+ADD = mybir.AluOpType.add
+SUB = mybir.AluOpType.subtract
+
+Z_CHUNKS = ((0, 512), (512, 768), (768, 1024))
+OUT_CHUNKS = ((0, 512), (512, 1024))
+LAST_CHUNKS = ((0, 512), (512, 768), (768, 1024))
+
+
+def entries(offsets, lo, hi):
+    return offsets[:, lo // 16 : hi // 16]
+
+
+def tile_picked_codepagemgap_none_p_kernel(
+    tc, x_words, x_scales, d_words, d_scales, mem, gs, offs, k1, n1, n2, k2, n3, n4, out
+):
+    nc = tc.nc
+    with ExitStack() as ctx:
+        lists = ctx.enter_context(tc.tile_pool(name="lists", bufs=1))
+        keep = ctx.enter_context(tc.tile_pool(name="keep", bufs=1))
+        psum = ctx.enter_context(tc.psum_pool(name="psum", bufs=8))
+
+        def load_list(name, src):
+            tile = lists.tile(list(src.shape), U16, name=name)
+            nc.sync.dma_start(tile[:], src)
+            return tile
+
+        d_scale_tab = keep.tile([P, G], U8, align_bytes=64)
+        x_scale_tab = keep.tile([P, T], U8, align_bytes=64)
+        d_word_tab = keep.tile([P, G], U32, align_bytes=64)
+        x_word_tab = keep.tile([P, T], U32, tag="x_word_tab", align_bytes=64)
+        nc.gpsimd.memset(d_scale_tab[:].bitcast(I32), 0)
+        nc.vector.memset(x_scale_tab[:].bitcast(I32), 0)
+
+        k1_t = load_list("k1_t", k1)
+        offs_t = load_list("offs_t", offs)
+        gain = keep.tile([P, PACK], F32)
+        nc.sync.dma_start(gain[:], gs.rearrange("(p t) o -> p (t o)", t=PACK))
+        k2_t = load_list("k2_t", k2)
+        n1_t = load_list("n1_t", n1)
+        nc.sync.dma_start(d_scale_tab[0:P:8, :].bitcast(I32), d_scales[0].bitcast(I32))
+        nc.sync.dma_start(x_scale_tab[0:P:8, :].bitcast(I32), x_scales[0].bitcast(I32))
+        nc.sync.dma_start(x_word_tab[:].bitcast(I32), x_words[0].rearrange("p n t -> p (n t)").bitcast(I32))
+        nc.sync.dma_start(d_word_tab[:].bitcast(I32), d_words[0].rearrange("p n t -> p (n t)").bitcast(I32))
+        mem_rows = mem.rearrange("(p t) w -> t p w", t=PACK)
+        out_rows = out.rearrange("(p t) w -> t p w", t=PACK)
+        page = []
+
+        def load_page(tag):
+            t = len(page)
+            page.append(keep.tile([P, U], F32, name="page%d" % t, tag=tag, align_bytes=64))
+            nc.sync.dma_start(page[t][:], mem_rows[t])
+
+        load_page("page0")
+        n2_t = load_list("n2_t", n2)
+        n4_t = load_list("n4_t", n4)
+        n3_t = load_list("n3_t", n3)
+
+        minus_half_gain = keep.tile([P, PACK], F32)
+        nc.scalar.activation(minus_half_gain[:], gain[:], COPY, scale=-0.5)
+
+        def deal(dst, src):
+            nc.vector.tensor_copy(dst.rearrange("p (t m) -> p m t", t=PACK), src.rearrange("p (m t) -> p m t", t=PACK))
+
+        def settle(planes):
+            for j in range(1, 4):
+                nc.scalar.dma_start(planes[j:P:32, :].bitcast(I32), planes[8 * j : P : 32, :].bitcast(I32))
+
+        def picked_words(name, offsets, tag):
+            got = keep.tile([P, H], U32, name=name + "_got", tag=tag, align_bytes=64)
+            nc.vector.tensor_copy(got[:], d_word_tab[:].indirect(offsets[:]))
+            dealt = keep.tile([P, H], U32, name=name + "_dealt", align_bytes=64)
+            deal(dealt[:], got[:])
+            return dealt
+
+        w1s_got = keep.tile([P, H], U8, tag="w1s_got", align_bytes=64)
+        nc.vector.tensor_copy(w1s_got[:], d_scale_tab[:].indirect(k1_t[:]))
+        xs_got = keep.tile([P, S], U8, tag="xs_got", align_bytes=64)
+        nc.vector.tensor_copy(xs_got[:], x_scale_tab[:].indirect(offs_t[:]))
+        first_planes = keep.tile([P, H + S], U8, align_bytes=64)
+        deal(first_planes[:, 0:H], w1s_got[:])
+        nc.vector.tensor_copy(first_planes[:, H : H + S].bitcast(I32), xs_got[:].bitcast(I32))
+        settle(first_planes)
+        w1_scales = first_planes[:, 0:H]
+        x_sc = first_planes[:, H : H + S]
+        load_page("w1s_got")
+        load_page("xs_got")
+        x_wd = keep.tile([P, S], U32, align_bytes=64)
+        nc.vector.tensor_copy(x_wd[:], x_word_tab[:].indirect(offs_t[:]))
+        load_page("x_word_tab")
+        w1_words = picked_words("w1w", k1_t, "w1w_got")
+        w2s_got = keep.tile([P, H], U8, tag="w1w_got", align_bytes=64)
+        nc.vector.tensor_copy(w2s_got[:], d_scale_tab[:].indirect(k2_t[:]))
+        w2_scales = keep.tile([P, H], U8, align_bytes=64)
+        deal(w2_scales[:], w2s_got[:])
+        settle(w2_scales)
+
+        halved, whole = [], []
+        for t in range(PACK):
+            cols = slice(P * t, P * (t + 1))
+            acc = psum.tile([P, 512], F32, name="acc", tag="acc")
+            nc.tensor.matmul_mx(
+                acc[:], lhsT=w1_words[:, cols].bitcast(FP8X4), lhsT_scale=w1_scales[:, cols],
+                rhs=x_wd[:].bitcast(FP8X4), rhs_scale=x_sc, start=True, stop=True,
+            )
+            h = keep.tile([P, S], F32, name="h%d" % t)
+            nc.scalar.activation(h[:], acc[:], COPY, scale=0.0625)
+            nc.vector.tensor_copy(page[t][:].indirect(n1_t[:]), h[:])
+            halved.append(keep.tile([P, U], F32, name="halved%d" % t))
+            nc.scalar.activation(halved[t][:], page[t][:], COPY, scale=minus_half_gain[:, t : t + 1])
+            whole.append(keep.tile([P, U], F32, name="whole%d" % t, tag="whole%d" % t, align_bytes=64))
+            nc.scalar.activation(whole[t][:], page[t][:], COPY, scale=gain[:, t : t + 1])
+
+        z_words = keep.tile([P, U], U32, align_bytes=64)
+        z_scales = keep.tile([P, U], U8, align_bytes=64)
+        woven = []
+        for c, (lo, hi) in enumerate(Z_CHUNKS):
+            z = keep.tile([P, PACK, hi - lo], F32, name="z%d" % c)
+            for t in range(PACK):
+                nc.vector.tensor_tensor(z[:, t, :], halved[t][:].indirect(entries(n2_t, lo, hi)), whole[t][:, lo:hi], ADD)
+            woven.append(keep.tile([P, hi - lo, PACK], BF16, name="woven%d" % c, align_bytes=64))
+            nc.scalar.copy(woven[c][:], z[:].rearrange("p t w -> p w t"))
+
+        def quantise(c):
+            lo, hi = Z_CHUNKS[c]
+            nc.vector.quantize_mx(
+                z_words[:, lo:hi].bitcast(FP8X4), z_scales[:, lo:hi], woven[c][:].rearrange("p w t -> p (w t)")
+            )
+
+        quantise(0)
+        w2_words = picked_words("w2w", k2_t, "whole3")
+        quantise(1)
+        quantise(2)
+
+        for t in range(PACK):
+            cols = slice(P * t, P * (t + 1))
+            h2 = keep.tile([P, U], F32, name="h2_%d" % t)
+            for lo, hi in Z_CHUNKS:
+                acc = psum.tile([P, 512], F32, name="acc", tag="acc")
+                nc.tensor.matmul_mx(
+                    acc[:, 0 : hi - lo], lhsT=w2_words[:, cols].bitcast(FP8X4), lhsT_scale=w2_scales[:, cols],
+                    rhs=z_words[:, lo:hi].bitcast(FP8X4), rhs_scale=z_scales[:, lo:hi], start=True, stop=True,
+                )
+                nc.scalar.activation(h2[:, lo:hi], acc[:, 0 : hi - lo], COPY, scale=0.0625)
+            chunks = LAST_CHUNKS if t == PACK - 1 else OUT_CHUNKS
+            less = keep.tile([P, U], F32, name="less%d" % t)
+            res = keep.tile([P, U], F32, name="res%d" % t)
+            for lo, hi in chunks:
+                nc.vector.tensor_copy(less[:, lo:hi], h2[:].indirect(entries(n4_t, lo, hi)))
+            for lo, hi in chunks:
+                nc.vector.tensor_tensor(res[:, lo:hi], h2[:].indirect(entries(n3_t, lo, hi)), less[:, lo:hi], SUB)
+                nc.sync.dma_start(out_rows[t][:, lo:hi], res[:, lo:hi])

@@ -16,9 +16,11 @@ U8 = mybir.dt.uint8
 FP8X4 = mybir.dt.float8_e4m3fn_x4
 COPY = mybir.ActivationFunctionType.Copy
 ADD = mybir.AluOpType.add
+MULT = mybir.AluOpType.mult
 SUB = mybir.AluOpType.subtract
 
 Z_CHUNKS = ((0, 512), (512, 768), (768, 1024))
+WHOLE_PARTS = (((0, 1024),), ((0, 1024),), Z_CHUNKS, ((0, 512), (512, 1024)))
 OUT_CHUNKS = ((0, 512), (512, 1024))
 LAST_CHUNKS = ((0, 512), (512, 768), (768, 1024))
 
@@ -34,6 +36,7 @@ def tile_picked_codepagemgap_none_p_kernel(
     with ExitStack() as ctx:
         lists = ctx.enter_context(tc.tile_pool(name="lists", bufs=1))
         keep = ctx.enter_context(tc.tile_pool(name="keep", bufs=1))
+        reused = ctx.enter_context(tc.tile_pool(name="reused", bufs=1))
         psum = ctx.enter_context(tc.psum_pool(name="psum", bufs=8))
 
         def load_list(name, src):
@@ -44,30 +47,29 @@ def tile_picked_codepagemgap_none_p_kernel(
         d_scale_tab = keep.tile([P, G], U8, align_bytes=64)
         x_scale_tab = keep.tile([P, T], U8, align_bytes=64)
         d_word_tab = keep.tile([P, G], U32, align_bytes=64)
-        x_word_tab = keep.tile([P, T], U32, tag="x_word_tab", align_bytes=64)
-        nc.gpsimd.memset(d_scale_tab[:].bitcast(I32), 0)
-        nc.vector.memset(x_scale_tab[:].bitcast(I32), 0)
+        x_word_tab = keep.tile([P, T], U32, align_bytes=64)
+        nc.vector.memset(d_scale_tab[:].bitcast(I32), 0)
+        nc.gpsimd.memset(x_scale_tab[:].bitcast(I32), 0)
 
         k1_t = load_list("k1_t", k1)
         offs_t = load_list("offs_t", offs)
         gain = keep.tile([P, PACK], F32)
         nc.sync.dma_start(gain[:], gs.rearrange("(p t) o -> p (t o)", t=PACK))
         k2_t = load_list("k2_t", k2)
-        n1_t = load_list("n1_t", n1)
         nc.sync.dma_start(d_scale_tab[0:P:8, :].bitcast(I32), d_scales[0].bitcast(I32))
         nc.sync.dma_start(x_scale_tab[0:P:8, :].bitcast(I32), x_scales[0].bitcast(I32))
         nc.sync.dma_start(x_word_tab[:].bitcast(I32), x_words[0].rearrange("p n t -> p (n t)").bitcast(I32))
         nc.sync.dma_start(d_word_tab[:].bitcast(I32), d_words[0].rearrange("p n t -> p (n t)").bitcast(I32))
+        n1_t = load_list("n1_t", n1)
         mem_rows = mem.rearrange("(p t) w -> t p w", t=PACK)
         out_rows = out.rearrange("(p t) w -> t p w", t=PACK)
         page = []
 
-        def load_page(tag):
-            t = len(page)
-            page.append(keep.tile([P, U], F32, name="page%d" % t, tag=tag, align_bytes=64))
-            nc.sync.dma_start(page[t][:], mem_rows[t])
+        def load_page(tile):
+            nc.sync.dma_start(tile[:], mem_rows[len(page)])
+            page.append(tile)
 
-        load_page("page0")
+        load_page(keep.tile([P, U], F32, name="page0"))
         n2_t = load_list("n2_t", n2)
         n4_t = load_list("n4_t", n4)
         n3_t = load_list("n3_t", n3)
@@ -82,36 +84,27 @@ def tile_picked_codepagemgap_none_p_kernel(
             for j in range(1, 4):
                 nc.scalar.dma_start(planes[j:P:32, :].bitcast(I32), planes[8 * j : P : 32, :].bitcast(I32))
 
-        def picked_words(name, offsets, tag):
-            got = keep.tile([P, H], U32, name=name + "_got", tag=tag, align_bytes=64)
-            nc.vector.tensor_copy(got[:], d_word_tab[:].indirect(offsets[:]))
-            dealt = keep.tile([P, H], U32, name=name + "_dealt", align_bytes=64)
-            deal(dealt[:], got[:])
-            return dealt
-
-        w1s_got = keep.tile([P, H], U8, tag="w1s_got", align_bytes=64)
+        w1s_got = keep.tile([P, H], U8, align_bytes=64)
         nc.vector.tensor_copy(w1s_got[:], d_scale_tab[:].indirect(k1_t[:]))
-        xs_got = keep.tile([P, S], U8, tag="xs_got", align_bytes=64)
+        xs_got = keep.tile([P, S], U8, align_bytes=64)
         nc.vector.tensor_copy(xs_got[:], x_scale_tab[:].indirect(offs_t[:]))
-        first_planes = keep.tile([P, H + S], U8, align_bytes=64)
+        first_planes = keep.tile([P, H + S], U8, tag="first_planes", align_bytes=64)
         deal(first_planes[:, 0:H], w1s_got[:])
         nc.vector.tensor_copy(first_planes[:, H : H + S].bitcast(I32), xs_got[:].bitcast(I32))
         settle(first_planes)
         w1_scales = first_planes[:, 0:H]
         x_sc = first_planes[:, H : H + S]
-        load_page("w1s_got")
-        load_page("xs_got")
-        x_wd = keep.tile([P, S], U32, align_bytes=64)
+        x_wd = keep.tile([P, S], U32, tag="x_wd", align_bytes=64)
         nc.vector.tensor_copy(x_wd[:], x_word_tab[:].indirect(offs_t[:]))
-        load_page("x_word_tab")
-        w1_words = picked_words("w1w", k1_t, "w1w_got")
-        w2s_got = keep.tile([P, H], U8, tag="w1w_got", align_bytes=64)
+        w1w_got = reused.tile([P, H], U32, offset=3072, align_bytes=64)
+        nc.vector.tensor_copy(w1w_got[:], d_word_tab[:].indirect(k1_t[:]))
+        w1_words = keep.tile([P, H], U32, align_bytes=64)
+        deal(w1_words[:], w1w_got[:])
+        load_page(reused.tile([P, U], F32, name="page1", offset=0, align_bytes=64))
+        w2s_got = reused.tile([P, H], U8, offset=4608, align_bytes=64)
         nc.vector.tensor_copy(w2s_got[:], d_scale_tab[:].indirect(k2_t[:]))
-        w2_scales = keep.tile([P, H], U8, align_bytes=64)
-        deal(w2_scales[:], w2s_got[:])
-        settle(w2_scales)
 
-        halved, whole = [], []
+        h = []
         for t in range(PACK):
             cols = slice(P * t, P * (t + 1))
             acc = psum.tile([P, 512], F32, name="acc", tag="acc")
@@ -119,45 +112,71 @@ def tile_picked_codepagemgap_none_p_kernel(
                 acc[:], lhsT=w1_words[:, cols].bitcast(FP8X4), lhsT_scale=w1_scales[:, cols],
                 rhs=x_wd[:].bitcast(FP8X4), rhs_scale=x_sc, start=True, stop=True,
             )
-            h = keep.tile([P, S], F32, name="h%d" % t)
-            nc.scalar.activation(h[:], acc[:], COPY, scale=0.0625)
-            nc.vector.tensor_copy(page[t][:].indirect(n1_t[:]), h[:])
+            h.append(keep.tile([P, S], F32, name="h%d" % t))
+            nc.scalar.activation(h[t][:], acc[:], COPY, scale=0.0625)
+
+        load_page(keep.tile([P, U], F32, name="page2", tag="x_wd", align_bytes=64))
+        load_page(keep.tile([P, U], F32, name="page3", tag="first_planes", align_bytes=64))
+        w2_scales = keep.tile([P, H], U8, align_bytes=64)
+        deal(w2_scales[:], w2s_got[:])
+        settle(w2_scales)
+
+        halved, whole = [], []
+        for t in range(PACK):
+            nc.vector.tensor_copy(page[t][:].indirect(n1_t[:]), h[t][:])
             halved.append(keep.tile([P, U], F32, name="halved%d" % t))
             nc.scalar.activation(halved[t][:], page[t][:], COPY, scale=minus_half_gain[:, t : t + 1])
-            whole.append(keep.tile([P, U], F32, name="whole%d" % t, tag="whole%d" % t, align_bytes=64))
-            nc.scalar.activation(whole[t][:], page[t][:], COPY, scale=gain[:, t : t + 1])
+            parts = []
+            for lo, hi in WHOLE_PARTS[t]:
+                part = keep.tile([P, hi - lo], F32, name="whole%d_%d" % (t, lo), tag="whole%d_%d" % (t, lo), align_bytes=64)
+                nc.scalar.activation(part[:], page[t][:, lo:hi], COPY, scale=gain[:, t : t + 1])
+                parts.extend(part[:, a - lo : b - lo] for a, b in Z_CHUNKS if lo <= a < hi)
+            whole.append(parts)
 
-        z_words = keep.tile([P, U], U32, align_bytes=64)
-        z_scales = keep.tile([P, U], U8, align_bytes=64)
-        woven = []
+        woven, z_words, z_scales = [], [], []
         for c, (lo, hi) in enumerate(Z_CHUNKS):
-            z = keep.tile([P, PACK, hi - lo], F32, name="z%d" % c)
+            z = keep.tile([P, PACK, hi - lo], F32, name="z%d" % c, tag=("z0", "whole3_0", "whole2_512")[c], align_bytes=64)
             for t in range(PACK):
-                nc.vector.tensor_tensor(z[:, t, :], halved[t][:].indirect(entries(n2_t, lo, hi)), whole[t][:, lo:hi], ADD)
-            woven.append(keep.tile([P, hi - lo, PACK], BF16, name="woven%d" % c, align_bytes=64))
+                nc.vector.tensor_tensor(z[:, t, :], halved[t][:].indirect(entries(n2_t, lo, hi)), whole[t][c], ADD)
+            woven.append(keep.tile([P, hi - lo, PACK], BF16, name="woven%d" % c, tag="woven%d" % c, align_bytes=64))
             nc.scalar.copy(woven[c][:], z[:].rearrange("p t w -> p w t"))
 
         def quantise(c):
             lo, hi = Z_CHUNKS[c]
+            z_words.append(keep.tile([P, hi - lo], U32, name="z_words%d" % c, align_bytes=64))
+            z_scales.append(keep.tile([P, hi - lo], U8, name="z_scales%d" % c, align_bytes=64))
             nc.vector.quantize_mx(
-                z_words[:, lo:hi].bitcast(FP8X4), z_scales[:, lo:hi], woven[c][:].rearrange("p w t -> p (w t)")
+                z_words[c][:].bitcast(FP8X4), z_scales[c][:], woven[c][:].rearrange("p w t -> p (w t)")
             )
 
+        w2w_got = keep.tile([P, H], U32, tag="whole2_768", align_bytes=64)
+        nc.vector.tensor_copy(w2w_got[:], d_word_tab[:].indirect(k2_t[:]))
         quantise(0)
-        w2_words = picked_words("w2w", k2_t, "whole3")
+        by_tile = w2w_got[:].rearrange("p (m t) -> p m t", t=PACK)
+        w2_first = keep.tile([P, P], U32, align_bytes=64)
+        nc.vector.tensor_copy(w2_first[:], by_tile[:, :, 0])
         quantise(1)
         quantise(2)
+        w2_rest = keep.tile([P, H - P], U32, tag="woven2", align_bytes=64)
+        nc.vector.tensor_copy(w2_rest[:].rearrange("p (t m) -> p m t", t=PACK - 1), by_tile[:, :, 1:PACK])
+        w2_words = [w2_first[:]] + [w2_rest[:, P * t : P * (t + 1)] for t in range(PACK - 1)]
 
         for t in range(PACK):
             cols = slice(P * t, P * (t + 1))
             h2 = keep.tile([P, U], F32, name="h2_%d" % t)
-            for lo, hi in Z_CHUNKS:
-                acc = psum.tile([P, 512], F32, name="acc", tag="acc")
-                nc.tensor.matmul_mx(
-                    acc[:, 0 : hi - lo], lhsT=w2_words[:, cols].bitcast(FP8X4), lhsT_scale=w2_scales[:, cols],
-                    rhs=z_words[:, lo:hi].bitcast(FP8X4), rhs_scale=z_scales[:, lo:hi], start=True, stop=True,
-                )
-                nc.scalar.activation(h2[:, lo:hi], acc[:, 0 : hi - lo], COPY, scale=0.0625)
+            width = 256 if t == 0 else 512
+            for c, (lo, hi) in enumerate(Z_CHUNKS):
+                for a in range(0, hi - lo, width):
+                    b = min(a + width, hi - lo)
+                    acc = psum.tile([P, 512], F32, name="acc", tag="acc")
+                    nc.tensor.matmul_mx(
+                        acc[:, 0 : b - a], lhsT=w2_words[t].bitcast(FP8X4), lhsT_scale=w2_scales[:, cols],
+                        rhs=z_words[c][:, a:b].bitcast(FP8X4), rhs_scale=z_scales[c][:, a:b], start=True, stop=True,
+                    )
+                    if t == 0 and hi == U:
+                        nc.vector.tensor_scalar(h2[:, lo + a : lo + b], acc[:, 0 : b - a], 0.0625, None, MULT)
+                    else:
+                        nc.scalar.activation(h2[:, lo + a : lo + b], acc[:, 0 : b - a], COPY, scale=0.0625)
             chunks = LAST_CHUNKS if t == PACK - 1 else OUT_CHUNKS
             less = keep.tile([P, U], F32, name="less%d" % t)
             res = keep.tile([P, U], F32, name="res%d" % t)

from contextlib import ExitStack

import concourse.mybir as mybir

K, T, S, G, H, U = 512, 1024, 512, 2048, 512, 1024
P = 128
PACK = 4
FLOPS = 2 * K * H * S + 2 * K * H * U

F32 = mybir.dt.float32
BF16 = mybir.dt.bfloat16
I32 = mybir.dt.int32
U32 = mybir.dt.uint32
U16 = mybir.dt.uint16
U8 = mybir.dt.uint8
FP8X4 = mybir.dt.float8_e4m3fn_x4
COPY = mybir.ActivationFunctionType.Copy
ADD = mybir.AluOpType.add
MULT = mybir.AluOpType.mult
SUB = mybir.AluOpType.subtract

Z_CHUNKS = ((0, 512), (512, 768), (768, 1024))
WHOLE_PARTS = (((0, 1024),), ((0, 1024),), Z_CHUNKS, ((0, 512), (512, 1024)))
OUT_CHUNKS = ((0, 512), (512, 1024))
LAST_CHUNKS = ((0, 512), (512, 768), (768, 1024))


def entries(offsets, lo, hi):
    return offsets[:, lo // 16 : hi // 16]


def tile_picked_codepagemgap_none_p_kernel(
    tc, x_words, x_scales, d_words, d_scales, mem, gs, offs, k1, n1, n2, k2, n3, n4, out
):
    nc = tc.nc
    with ExitStack() as ctx:
        lists = ctx.enter_context(tc.tile_pool(name="lists", bufs=1))
        keep = ctx.enter_context(tc.tile_pool(name="keep", bufs=1))
        reused = ctx.enter_context(tc.tile_pool(name="reused", bufs=1))
        psum = ctx.enter_context(tc.psum_pool(name="psum", bufs=8))

        def load_list(name, src):
            tile = lists.tile(list(src.shape), U16, name=name)
            nc.sync.dma_start(tile[:], src)
            return tile

        d_scale_tab = keep.tile([P, G], U8, align_bytes=64)
        x_scale_tab = keep.tile([P, T], U8, align_bytes=64)
        d_word_tab = keep.tile([P, G], U32, align_bytes=64)
        x_word_tab = keep.tile([P, T], U32, align_bytes=64)
        nc.vector.memset(d_scale_tab[:].bitcast(I32), 0)
        nc.gpsimd.memset(x_scale_tab[:].bitcast(I32), 0)

        k1_t = load_list("k1_t", k1)
        offs_t = load_list("offs_t", offs)
        gain = keep.tile([P, PACK], F32)
        nc.sync.dma_start(gain[:], gs.rearrange("(p t) o -> p (t o)", t=PACK))
        k2_t = load_list("k2_t", k2)
        nc.sync.dma_start(d_scale_tab[0:P:8, :].bitcast(I32), d_scales[0].bitcast(I32))
        nc.sync.dma_start(x_scale_tab[0:P:8, :].bitcast(I32), x_scales[0].bitcast(I32))
        nc.sync.dma_start(x_word_tab[:].bitcast(I32), x_words[0].rearrange("p n t -> p (n t)").bitcast(I32))
        nc.sync.dma_start(d_word_tab[:].bitcast(I32), d_words[0].rearrange("p n t -> p (n t)").bitcast(I32))
        n1_t = load_list("n1_t", n1)
        mem_rows = mem.rearrange("(p t) w -> t p w", t=PACK)
        out_rows = out.rearrange("(p t) w -> t p w", t=PACK)
        page = []

        def load_page(tile):
            nc.sync.dma_start(tile[:], mem_rows[len(page)])
            page.append(tile)

        load_page(keep.tile([P, U], F32, name="page0"))
        n2_t = load_list("n2_t", n2)
        n4_t = load_list("n4_t", n4)
        n3_t = load_list("n3_t", n3)

        minus_half_gain = keep.tile([P, PACK], F32)
        nc.scalar.activation(minus_half_gain[:], gain[:], COPY, scale=-0.5)

        def deal(dst, src):
            nc.vector.tensor_copy(dst.rearrange("p (t m) -> p m t", t=PACK), src.rearrange("p (m t) -> p m t", t=PACK))

        def settle(planes):
            for j in range(1, 4):
                nc.scalar.dma_start(planes[j:P:32, :].bitcast(I32), planes[8 * j : P : 32, :].bitcast(I32))

        w1s_got = keep.tile([P, H], U8, align_bytes=64)
        nc.vector.tensor_copy(w1s_got[:], d_scale_tab[:].indirect(k1_t[:]))
        xs_got = keep.tile([P, S], U8, align_bytes=64)
        nc.vector.tensor_copy(xs_got[:], x_scale_tab[:].indirect(offs_t[:]))
        first_planes = keep.tile([P, H + S], U8, tag="first_planes", align_bytes=64)
        deal(first_planes[:, 0:H], w1s_got[:])
        nc.vector.tensor_copy(first_planes[:, H : H + S].bitcast(I32), xs_got[:].bitcast(I32))
        settle(first_planes)
        w1_scales = first_planes[:, 0:H]
        x_sc = first_planes[:, H : H + S]
        x_wd = keep.tile([P, S], U32, tag="x_wd", align_bytes=64)
        nc.vector.tensor_copy(x_wd[:], x_word_tab[:].indirect(offs_t[:]))
        w1w_got = reused.tile([P, H], U32, offset=3072, align_bytes=64)
        nc.vector.tensor_copy(w1w_got[:], d_word_tab[:].indirect(k1_t[:]))
        w1_words = keep.tile([P, H], U32, align_bytes=64)
        deal(w1_words[:], w1w_got[:])
        load_page(reused.tile([P, U], F32, name="page1", offset=0, align_bytes=64))
        w2s_got = reused.tile([P, H], U8, offset=4608, align_bytes=64)
        nc.vector.tensor_copy(w2s_got[:], d_scale_tab[:].indirect(k2_t[:]))

        h = []
        for t in range(PACK):
            cols = slice(P * t, P * (t + 1))
            acc = psum.tile([P, 512], F32, name="acc", tag="acc")
            nc.tensor.matmul_mx(
                acc[:], lhsT=w1_words[:, cols].bitcast(FP8X4), lhsT_scale=w1_scales[:, cols],
                rhs=x_wd[:].bitcast(FP8X4), rhs_scale=x_sc, start=True, stop=True,
            )
            h.append(keep.tile([P, S], F32, name="h%d" % t))
            nc.scalar.activation(h[t][:], acc[:], COPY, scale=0.0625)

        load_page(keep.tile([P, U], F32, name="page2", tag="x_wd", align_bytes=64))
        load_page(keep.tile([P, U], F32, name="page3", tag="first_planes", align_bytes=64))
        w2_scales = keep.tile([P, H], U8, align_bytes=64)
        deal(w2_scales[:], w2s_got[:])
        settle(w2_scales)

        halved, whole = [], []
        for t in range(PACK):
            nc.vector.tensor_copy(page[t][:].indirect(n1_t[:]), h[t][:])
            halved.append(keep.tile([P, U], F32, name="halved%d" % t))
            nc.scalar.activation(halved[t][:], page[t][:], COPY, scale=minus_half_gain[:, t : t + 1])
            parts = []
            for lo, hi in WHOLE_PARTS[t]:
                part = keep.tile([P, hi - lo], F32, name="whole%d_%d" % (t, lo), tag="whole%d_%d" % (t, lo), align_bytes=64)
                nc.scalar.activation(part[:], page[t][:, lo:hi], COPY, scale=gain[:, t : t + 1])
                parts.extend(part[:, a - lo : b - lo] for a, b in Z_CHUNKS if lo <= a < hi)
            whole.append(parts)

        woven, z_words, z_scales = [], [], []
        for c, (lo, hi) in enumerate(Z_CHUNKS):
            z = keep.tile([P, PACK, hi - lo], F32, name="z%d" % c, tag=("z0", "whole3_0", "whole2_512")[c], align_bytes=64)
            for t in range(PACK):
                nc.vector.tensor_tensor(z[:, t, :], halved[t][:].indirect(entries(n2_t, lo, hi)), whole[t][c], ADD)
            woven.append(keep.tile([P, hi - lo, PACK], BF16, name="woven%d" % c, tag="woven%d" % c, align_bytes=64))
            nc.scalar.copy(woven[c][:], z[:].rearrange("p t w -> p w t"))

        def quantise(c):
            lo, hi = Z_CHUNKS[c]
            z_words.append(keep.tile([P, hi - lo], U32, name="z_words%d" % c, align_bytes=64))
            z_scales.append(keep.tile([P, hi - lo], U8, name="z_scales%d" % c, align_bytes=64))
            nc.vector.quantize_mx(
                z_words[c][:].bitcast(FP8X4), z_scales[c][:], woven[c][:].rearrange("p w t -> p (w t)")
            )

        w2w_got = keep.tile([P, H], U32, tag="whole2_768", align_bytes=64)
        nc.vector.tensor_copy(w2w_got[:], d_word_tab[:].indirect(k2_t[:]))
        quantise(0)
        by_tile = w2w_got[:].rearrange("p (m t) -> p m t", t=PACK)
        w2_first = keep.tile([P, P], U32, align_bytes=64)
        nc.vector.tensor_copy(w2_first[:], by_tile[:, :, 0])
        quantise(1)
        quantise(2)
        w2_rest = keep.tile([P, H - P], U32, tag="woven2", align_bytes=64)
        nc.vector.tensor_copy(w2_rest[:].rearrange("p (t m) -> p m t", t=PACK - 1), by_tile[:, :, 1:PACK])
        w2_words = [w2_first[:]] + [w2_rest[:, P * t : P * (t + 1)] for t in range(PACK - 1)]

        for t in range(PACK):
            cols = slice(P * t, P * (t + 1))
            h2 = keep.tile([P, U], F32, name="h2_%d" % t)
            width = 256 if t == 0 else 512
            for c, (lo, hi) in enumerate(Z_CHUNKS):
                for a in range(0, hi - lo, width):
                    b = min(a + width, hi - lo)
                    acc = psum.tile([P, 512], F32, name="acc", tag="acc")
                    nc.tensor.matmul_mx(
                        acc[:, 0 : b - a], lhsT=w2_words[t].bitcast(FP8X4), lhsT_scale=w2_scales[:, cols],
                        rhs=z_words[c][:, a:b].bitcast(FP8X4), rhs_scale=z_scales[c][:, a:b], start=True, stop=True,
                    )
                    if t == 0 and hi == U:
                        nc.vector.tensor_scalar(h2[:, lo + a : lo + b], acc[:, 0 : b - a], 0.0625, None, MULT)
                    else:
                        nc.scalar.activation(h2[:, lo + a : lo + b], acc[:, 0 : b - a], COPY, scale=0.0625)
            chunks = LAST_CHUNKS if t == PACK - 1 else OUT_CHUNKS
            less = keep.tile([P, U], F32, name="less%d" % t)
            res = keep.tile([P, U], F32, name="res%d" % t)
            for lo, hi in chunks:
                nc.vector.tensor_copy(less[:, lo:hi], h2[:].indirect(entries(n4_t, lo, hi)))
            for lo, hi in chunks:
                nc.vector.tensor_tensor(res[:, lo:hi], h2[:].indirect(entries(n3_t, lo, hi)), less[:, lo:hi], SUB)
                nc.sync.dma_start(out_rows[t][:, lo:hi], res[:, lo:hi])
